import numpy as np, ml_dtypes
CORES = [1,5,17,21,33,37,49,53]
N = 8
import mx_ref
BF = ml_dtypes.bfloat16
def entries(a):
    return np.ascontiguousarray(a.T).reshape(-1)
def table(e):
    return np.ascontiguousarray(np.reshape(e, (-1, 16)).T).astype(np.int32)
def cols(t, e):
    v = np.concatenate([t.reshape(128, -1, 4), np.zeros((128, 1, 4), BF)], axis=1)
    return np.ascontiguousarray(v[:, e]).reshape(128, -1)
def cut(t, i, w=512):
    return t[:, w * i:w * i + w]
def f(rng, *shape):
    return mx_ref.flush((rng.standard_normal(shape, dtype=np.float32) * np.exp2(rng.integers(-2, 3, shape[:-1] + (1,)))).astype(BF))
def wide(rng, *shape, cols=0):
    v = rng.standard_normal(shape, dtype=np.float32) * np.exp2(rng.integers(-12, 13, shape)).astype(np.float32)
    if cols: v *= np.repeat(np.exp2(rng.integers(-cols, cols + 1, shape[:-2] + (1, shape[-1] // 4))) * (rng.random(shape[:-2] + (1, shape[-1] // 4)) > 0.0625), 4, axis=-1).astype(np.float32)
    return mx_ref.flush(v.astype(BF))
C, R, CAPP = 256, 3, 32
def lists(rng, full=False, stay=False, fresh=False, one=False):
    sl = np.full((N, R, N, CAPP), -1); pa = rng.integers(0, C, (N, R, C))
    for t in range(R):
        if stay: continue
        for r in range(N):
            for d in range(N):
                if d == r: continue
                n = CAPP if full else rng.integers(0, CAPP + 1)
                sl[r, t, d, rng.permutation(CAPP)[:n]] = rng.integers(0, C, n)
        for d in range(N):
            far = C + np.flatnonzero(sl[:, t, d].reshape(-1) >= 0)
            pa[d, t, rng.permutation(C)[:far.size]] = far
            if full: continue
            if far.size: pa[d, t, rng.integers(0, C, C // 16)] = rng.choice(far, C // 16)
            pa[d, t, rng.permutation(C)[:C // 2 if fresh else C // 8]] = -1
    if fresh: pa[rng.integers(0, N), rng.integers(0, R)] = -1
    if one:
        o, j = rng.integers(0, N), rng.integers(0, C)
        for t in range(R - 1):
            q, c, k = (o + rng.integers(1, N)) % N, rng.integers(0, CAPP), rng.integers(0, C)
            sl[o, t, q, c] = j; pa[q, t, k] = C + o * CAPP + c
            o, j = q, k
        for q in range(N):
            c = rng.integers(0, CAPP)
            if q != o: sl[o, R - 1, q, c] = j
            pa[q, R - 1] = j if q == o else C + o * CAPP + c
    return {"sl": np.stack([table(sl[r]) for r in range(N)]), "pa": np.stack([table(pa[r]) for r in range(N)])}
def setup_inputs(rng):
    return {"x": f(rng, N, 128, 4 * C * (R + 1)), "w": f(rng, N, 128, 512 * (R + 1)), **lists(rng)}
def setup_inputs_stay(rng):
    return {**setup_inputs(rng), **lists(rng, stay=True)}
def setup_inputs_far(rng):
    return {**setup_inputs(rng), **lists(rng, full=True)}
def setup_inputs_one(rng):
    return {**setup_inputs(rng), **lists(rng, one=True)}
def setup_inputs_fresh(rng):
    return {**setup_inputs(rng), **lists(rng, fresh=True)}
def setup_inputs_spread(rng):
    d = setup_inputs(rng); d["x"] = wide(rng, N, 128, 4 * C * (R + 1), cols=8); return d
def check_inputs(d):
    b = []
    s = [entries(d["sl"][r]).reshape(R, N, CAPP) for r in range(N)]
    for r in range(N):
        p = entries(d["pa"][r]).reshape(R, C)
        if s[r].min() < -1 or s[r].max() >= C or (s[r][:, r] != -1).any(): b.append("sl")
        if p.min() < -1 or p.max() >= C + N * CAPP: b.append("pa"); continue
        for t in range(R):
            slots = np.concatenate([s[q][t, r] for q in range(N)])
            if (slots[p[t][p[t] >= C] - C] < 0).any(): b.append("pa"); break
    return b
def reference(x, w, sl, pa):
    s = [entries(sl[r]).reshape(R, N, CAPP) for r in range(N)]
    p = [entries(pa[r]).reshape(R, C) for r in range(N)]
    cache = [np.ascontiguousarray(cut(x[r], 0, 4 * C)) for r in range(N)]
    y = np.zeros((N, 128, C * (R + 1)), np.float32)
    for t in range(R + 1):
        if t > 0:
            after = []
            for r in range(N):
                slots = [cols(cache[q], s[q][t - 1, r]) for q in range(N)]
                every = np.concatenate([cache[r]] + slots + [cut(x[r], t, 4 * C)], axis=1)
                v = p[r][t - 1]
                after.append(cols(every, np.where(v < 0, C + N * CAPP + np.arange(C), v)))
            cache = after
        for r in range(N):
            y[r][:, C * t:C * t + C] = mx_ref.matmul(mx_ref.quantize(np.ascontiguousarray(cut(w[r], t))), mx_ref.quantize(cache[r]))
    return {"y": y}

@@ -1,0 +1,285 @@
+from concourse.bass import DstId, RemoteDMATransfer
+from concourse.mybir import dt, AluOpType, ActivationFunctionType
+
+F8 = "float8_e4m3fn_x4"
+CW, SLOT = 256, 32
+NO = CW // 16
+WS = 2
+LIFT, DROP = 4096.0, 1048576.0
+
+SCRATCH = {
+    "WB": ("sbuf", [128, 2048], "bfloat16"),
+    "WQ": ("sbuf", [128, 512], F8), "WP": ("sbuf", [128, 512], "uint8"),
+    "KA": ("sbuf", [128, CW], F8), "PA": ("sbuf", [128, CW], "uint8"),
+    "SLI": ("sbuf", [128, 48], "int32"), "PAI": ("sbuf", [128, 48], "int32"),
+    "OS": ("sbuf", [128, 48], "uint16"),
+    "OP": ("sbuf", [128, 48], "uint16"),
+    "pi": ("sbuf", [128, 2], "int32"), "pm": ("sbuf", [128, 2], "int32"), "pf": ("sbuf", [128, 2], "float32"),
+    "lf": ("sbuf", [128, 2], "float32"),
+    "J16": ("sbuf", [128, CW], "float32"), "mask": ("sbuf", [128, CW], "float32"), "step": ("sbuf", [128, CW], "float32"),
+    "BJ": ("sbuf", [128, 48], "int32"), "BJ2": ("sbuf", [128, 48], "int32"),
+    "neg": ("sbuf", [128, 48], "int32"), "new": ("sbuf", [128, 48], "int32"), "par": ("sbuf", [128, 48], "int32"),
+    "IW": ("sbuf", [128, 768], "float32"),
+    "Z": ("sbuf", [128, 768], "float32"),
+}
+for _t in range(4):
+    SCRATCH["X%d" % _t] = ("sbuf", [128, 1024], "bfloat16")
+    SCRATCH["Y%d" % _t] = ("sbuf", [128, 256], "float32")
+for _t in (1, 2, 3):
+    SCRATCH["W%d" % _t] = ("sbuf", [128, 768], F8)
+    SCRATCH["P%d" % _t] = ("sbuf", [128, 768], "uint8")
+    SCRATCH["S%d" % _t] = ("sbuf", [128, CW], F8)
+    SCRATCH["SS%d" % _t] = ("sbuf", [128, CW], "uint8")
+for _t in (2, 3):
+    SCRATCH["RP%d" % _t] = ("sbuf", [128, CW], "float32")
+    SCRATCH["CM%d" % _t] = ("sbuf", [128, CW], "float32")
+    SCRATCH["SC%d" % _t] = ("sbuf", [128, CW], "float32")
+    SCRATCH["CO%d" % _t] = ("sbuf", [128, NO], "uint16")
+for _t in range(7):
+    SCRATCH["ps%d" % _t] = ("psum", [128, 512], "float32")
+
+SEMAPHORES = (["lsl", "lpa", "lwa", "lwb", "lx0", "lx1", "lx2", "lx3"]
+              + ["%s%d" % (n, t) for n in ("ac", "as") for t in (1, 2, 3)]
+              + ["%s%d%d" % (n, t, k) for n in ("lc", "ls") for t in (1, 2, 3) for k in range(3)]
+              + ["e%d" % i for i in range(100)])
+
+
+def plan(T, topo, src, t):
+    chips = []
+    for d in T.cores:
+        if topo.chip(d) not in chips:
+            chips.append(topo.chip(d))
+    n, own = len(chips), chips.index(topo.chip(src))
+    far = [[T.rank_of(d) for d in T.cores if topo.chip(d) == chips[(own + k) % n]] for k in (2, 1, 3)]
+    peer = [d for d in T.cores if d != src and topo.chip(d) == topo.chip(src)][0]
+    eng = topo.engines(src, T.cores[far[0][0]])
+    even, odd = eng[0::2], eng[1::2]
+    near = [e for e in topo.engines(src, peer) if e not in eng]
+    p = {T.rank_of(peer): [near[0], near[2]]}
+
+    def one(gr):
+        return {gr[0]: even, gr[1]: odd}
+
+    def two(g1, g2):
+        m = len(even) // 2
+        return {g1[0]: even[:m], g1[1]: even[m:], g2[0]: odd[:m], g2[1]: odd[m:]}
+
+    steps = [far[0], far[1], far[2] + list(p)]
+    codes = [one(far[0]), one(far[1]), {**one(far[2]), **p}]
+    if t < 3:
+        scales = [one(far[0]), {**two(far[1], far[2]), **p}]
+    else:
+        scales = [two(far[0], far[1]), {**one(far[2]), **p}]
+    return steps, codes, scales
+
+
+def runs(ranks, own):
+    out = []
+    for d in sorted(ranks):
+        if out and (d == out[-1][1] or (d == out[-1][1] + 1 and out[-1][1] == own)):
+            out[-1][1] = d + 1
+        else:
+            out.append([d, d + 1])
+    return out
+
+
+def bits(engines):
+    m = 0
+    for e in engines:
+        m |= 1 << e
+    return m
+
+
+def rank_program(g, core, T, topo):
+    r = T.rank_of(core)
+    if r is None:
+        return
+    qs = {"g": g, "v": g.vector, "a": g.scalar, "t": g.tensor, "s": g.sync}
+    total, waited, count = {}, {}, [0]
+    Copy, Ident = ActivationFunctionType.Copy, ActivationFunctionType.Identity
+
+    def wait(q, *names):
+        for n in names:
+            if waited.get((q, n)) != total[n]:
+                qs[q].wait_ge(T.sem[n], total[n])
+                waited[(q, n)] = total[n]
+
+    def did(ins, n=1, name=None):
+        if name is None:
+            name = "e%d" % count[0]
+            count[0] += 1
+        ins.then_inc(T.sem[name], n)
+        total[name] = total.get(name, 0) + n
+        return name
+
+    def pickc(src, hi, off, dst, a, b, deps):
+        wait("v", *deps)
+        return did(g.vector.tensor_copy(dst[:, a:b].bitcast(dt.uint32), src[:, 0:hi].bitcast(dt.uint32).indirect(off)))
+
+    def picks(src, hi, off, dst, a, b, deps):
+        wait("a", *deps)
+        return did(g.scalar.activation(dst[:, a:b], src[:, 0:hi].indirect(off), Copy))
+
+    def dma(q, dst, src, name=None, after=()):
+        wait(q, *after)
+        return did(qs[q].dma_start(dst, src), 16, name)
+
+    mine = {t: plan(T, topo, core, t) for t in (1, 2, 3)}
+    for t in (1, 2, 3):
+        for arr, loc, part in (("ac", "lc", 1), ("as", "ls", 2)):
+            total["%s%d" % (arr, t)] = sum(len(c[r]) for s in T.cores if s != core
+                                           for c in plan(T, topo, s, t)[part] if r in c)
+            for k, c in enumerate(mine[t][part]):
+                total["%s%d%d" % (loc, t, k)] = sum(len(e) for e in c.values())
+    at = CW + SLOT * r
+
+    def exchange(t, part, win, hi, off, deps):
+        pick, dst, land, arr, loc = ((pickc, T["S%d" % t], T["W%d" % t], "ac", "lc"),
+                                     (picks, T["SS%d" % t], T["P%d" % t], "as", "ls"))[part]
+        for k, c in enumerate(mine[t][part + 1]):
+            ready = []
+            for st in mine[t][0]:
+                if st[0] in c:
+                    for a, b in runs(st, r):
+                        ready.append(pick(win, hi, off[:, 2 * a:2 * b], dst, SLOT * a, SLOT * b, deps))
+            trs = []
+            for d, e in c.items():
+                rid, pid, _ = topo.addr(T.cores[d])
+                s, w = dst[:, SLOT * d:SLOT * d + SLOT], land[:, at:at + SLOT]
+                if part == 0:
+                    s, w = s.bitcast(dt.uint8), w.bitcast(dt.uint8)
+                trs.append(RemoteDMATransfer(dst_ids=[DstId(rid=rid, pnc=pid)], dma_engine_mask=bits(e),
+                                             remote_sem=T.sem["%s%d" % (arr, t)], src=s, dst=w))
+            wait("g", *ready)
+            g.remote_dma_fused(trs, local_sem=T.sem["%s%d%d" % (loc, t, k)])
+
+    dma("s", T.X0[:, :], T.x[:, 0:1024], "lx0")
+    for i in range(8):
+        dma("a" if i < 4 else "s", T.SLI[16 * i:16 * i + 16, :], T.sl[:, :], "lsl")
+    for i in range(8):
+        dma("a" if i < 2 else "s", T.PAI[16 * i:16 * i + 16, :], T.pa[:, :], "lpa")
+    dma("s", T.X1[:, :], T.x[:, 1024:2048], "lx1")
+    dma("s", T.X2[:, :], T.x[:, 2048:3072], "lx2")
+    dma("s", T.X3[:, :], T.x[:, 3072:4096], "lx3", ["lx0"])
+
+    i_pi = did(g.iota(T.pi[:, 0:1], [[0, 1]], 0, 1))
+    i_w = did(g.iota(T.IW[:, 0:256], [[1, 256]], 0, 0, allow_small_or_imprecise_dtypes=True))
+    i_b = did(g.iota(T.BJ[:, :], [[0, 3], [16, 16]], 512, 0))
+    i_j16 = did(g.iota(T.J16[:, :], [[0, NO], [1, 16]], 0, 0, allow_small_or_imprecise_dtypes=True))
+    wait("a", i_w)
+    i_w1 = did(g.scalar.activation(T.IW[:, 256:512], T.IW[:, 0:256], Ident, bias=256.0))
+    i_w2 = did(g.scalar.activation(T.IW[:, 512:768], T.IW[:, 0:256], Ident, bias=512.0))
+    wait("v", i_pi)
+    v_pm = did(g.vector.tensor_scalar(T.pm[:, 0:1], T.pi[:, 0:1], 15, None, AluOpType.bitwise_and))
+    wait("v", v_pm)
+    v_pf = did(g.vector.tensor_copy(T.pf[:, 0:1], T.pm[:, 0:1]))
+    v_lf = did(g.vector.tensor_scalar(T.lf[:, 0:1], T.pm[:, 0:1], -LIFT, 15 * LIFT, AluOpType.mult, AluOpType.add))
+    wait("v", i_b, v_pf)
+    n0 = did(g.vector.tensor_scalar(T.BJ2[:, :], T.BJ[:, :], T.pf[:, 0:1], None, AluOpType.add))
+
+    wait("v", "lx0")
+    k0 = did(g.vector.quantize_mx(T.KA[:, :], T.PA[:, :], T.X0[:, :]))
+    wait("v", "lsl")
+    os_ = did(g.vector.tensor_copy(T.OS[:, :], T.SLI[:, :]))
+    exchange(1, 0, T.KA, CW, T.OS[:, 0:NO], [os_, k0])
+    exchange(1, 1, T.PA, CW, T.OS[:, 0:NO], [os_, k0])
+
+    wait("v", "lpa")
+    n1 = did(g.vector.tensor_scalar(T.neg[:, :], T.PAI[:, :], 0, None, AluOpType.is_lt))
+    wait("v", n0, n1)
+    n2 = did(g.vector.tensor_tensor(T.new[:, :], T.neg[:, :], T.BJ2[:, :], AluOpType.mult))
+    wait("v", n2)
+    n3 = did(g.vector.tensor_tensor(T.par[:, :], T.new[:, :], T.PAI[:, :], AluOpType.max))
+    wait("v", n3)
+    pa = did(g.vector.tensor_copy(T.OP[:, :], T.par[:, :]))
+    wait("v", i_j16)
+    v_mask = did(g.vector.tensor_scalar(T.mask[:, :], T.J16[:, :], T.pf[:, 0:1], -DROP, AluOpType.is_equal, AluOpType.mult))
+    wait("v", v_mask)
+    v_step = did(g.vector.tensor_scalar(T.step[:, :], T.mask[:, :], LIFT, None, AluOpType.add))
+    q0 = did(g.vector.quantize_mx(T.W1[:, 0:256], T.P1[:, 0:256], T.X0[:, :]))
+    wait("v", "lx1")
+    x1 = did(g.vector.quantize_mx(T.W1[:, 512:768], T.P1[:, 512:768], T.X1[:, :]))
+
+    def compose_a(t):
+        wait("a", pa, os_, i_w, i_w1, i_w2)
+        e = did(g.scalar.activation(T["RP%d" % t][:, :], T.IW[:, 0:768].indirect(T.OP[:, 16 * (t - 2):16 * (t - 1)]), Copy))
+        wait("a", e)
+        return did(g.scalar.activation(T["CM%d" % t][:, :], T["RP%d" % t][:, :].indirect(T.OS[:, NO * (t - 1):NO * t]), Copy))
+
+    def compose_v(t, e):
+        wait("v", e, v_step)
+        b = did(g.vector.tensor_tensor_scan(T["SC%d" % t][:, :], T.step[:, :], T["CM%d" % t][:, :], 0.0,
+                                            AluOpType.add, AluOpType.max))
+        wait("v", b, v_lf)
+        return did(g.vector.tensor_scalar(T["CO%d" % t][:, :], T["SC%d" % t][:, 15:CW:16], T.lf[:, 0:1], None, AluOpType.subtract))
+
+    co2 = compose_v(2, compose_a(2))
+    ca3 = compose_a(3)
+    own = T.OS[:, 2 * r:2 * r + 2]
+    fc = pickc(T.KA, CW, own, T.W3, at, at + SLOT, [os_, k0])
+    fs = picks(T.PA, CW, own, T.P3, at, at + SLOT, [os_, k0])
+    dma("s", T.WB[:, 0:512 * WS], T.w[:, 0:512 * WS], "lwa", ["lc12"])
+
+    d = [q0, x1, co2]
+    exchange(2, 0, T.W1, 768, T.CO2, d + ["ac1"])
+    exchange(2, 1, T.P1, 768, T.CO2, d + ["as1"])
+
+    k1c = pickc(T.W1, 768, T.OP[:, 0:16], T.W2, 0, CW, [pa, "ac1", q0, x1])
+    wait("v", "lx2")
+    x2 = did(g.vector.quantize_mx(T.W2[:, 512:768], T.P2[:, 512:768], T.X2[:, :]))
+    co3 = compose_v(3, ca3)
+    k1s = picks(T.P1, 768, T.OP[:, 0:16], T.P2, 0, CW, [pa, "as1", q0, x1])
+    dma("s", T.WB[:, 512 * WS:2048], T.w[:, 512 * WS:2048], "lwb", ["lc20"])
+
+    exchange(3, 0, T.W2, 768, T.CO3, [k1c, x2, co3, "ac2"])
+    exchange(3, 1, T.P2, 768, T.CO3, [k1s, x2, co3, "as2"])
+
+    k2c = pickc(T.W2, 768, T.OP[:, 16:32], T.W3, 0, CW, [pa, "ac2", k1c, x2])
+    k2s = picks(T.P2, 768, T.OP[:, 16:32], T.P3, 0, CW, [pa, "as2", k1s, x2])
+    wait("v", "lwa")
+    wqa = did(g.vector.quantize_mx(T.WQ[:, 0:128 * WS], T.WP[:, 0:128 * WS], T.WB[:, 0:512 * WS]))
+    wait("v", "lx3")
+    x3 = did(g.vector.quantize_mx(T.W3[:, 512:768], T.P3[:, 512:768], T.X3[:, :]))
+    wait("v", "lwb")
+    wqb = did(g.vector.quantize_mx(T.WQ[:, 128 * WS:512], T.WP[:, 128 * WS:512], T.WB[:, 512 * WS:2048]))
+
+    def product(ps, wt, win, pl, a, b, deps):
+        wait("t", wqa if wt < WS else wqb, *deps)
+        return did(g.tensor.matmul_mx(T["ps%d" % ps][:, 0:b - a], T.WQ[:, 128 * wt:128 * wt + 128], T.WP[:, 128 * wt:128 * wt + 128],
+                                      win[:, a:b], pl[:, a:b], True, True))
+
+    m0 = product(0, 0, T.W1, T.P1, 0, 256, [q0])
+    m1 = product(1, 1, T.W2, T.P2, 0, 256, [k1c, k1s])
+    mo = product(3, 3, T.W3, T.P3, 0, 256, [k2c, k2s])
+    mn = product(4, 3, T.W3, T.P3, 512, 768, [x3])
+    m2 = product(2, 2, T.W3, T.P3, 0, 256, [k2c, k2s])
+    wait("a", m0)
+    y0 = did(g.scalar.activation(T.Y0[:, :], T.ps0[:, 0:256], Copy))
+    wait("v", m1)
+    y1 = did(g.vector.tensor_copy(T.Y1[:, :], T.ps1[:, 0:256]))
+    wait("a", mo)
+    zo = did(g.scalar.activation(T.Z[:, 0:256], T.ps3[:, 0:256], Copy))
+    wait("v", mn)
+    zn = did(g.vector.tensor_copy(T.Z[:, 512:768], T.ps4[:, 0:256]))
+    wait("a", m2)
+    y2 = did(g.scalar.activation(T.Y2[:, :], T.ps2[:, 0:256], Copy))
+    st = [dma("s", T.y[:, 0:256], T.Y0[:, :], None, [y0, "lc32"]),
+          dma("s", T.y[:, 256:512], T.Y1[:, :], None, [y1]),
+          dma("s", T.y[:, 512:768], T.Y2[:, :], None, [y2])]
+
+    ma = product(5, 3, T.W3, T.P3, 256, 384, ["ac3", "as3", fc, fs])
+    mb = product(6, 3, T.W3, T.P3, 384, 512, ["ac3", "as3", fc, fs])
+    wait("a", ma)
+    za = did(g.scalar.activation(T.Z[:, 256:384], T.ps5[:, 0:128], Copy))
+    wait("v", mb)
+    zb = did(g.vector.tensor_copy(T.Z[:, 384:512], T.ps6[:, 0:128]))
+    wait("v", pa, zo, zn, za, zb)
+    fa = did(g.vector.tensor_copy(T.Y3[:, 0:128], T.Z[:, 0:768].indirect(T.OP[:, 32:40])))
+    wait("a", pa, zo, zn, za, zb)
+    fb = did(g.scalar.activation(T.Y3[:, 128:256], T.Z[:, 0:768].indirect(T.OP[:, 40:48]), Copy))
+    st.append(dma("s", T.y[:, 768:896], T.Y3[:, 0:128], None, [fa]))
+    st.append(dma("a", T.y[:, 896:1024], T.Y3[:, 128:256], None, [fb]))
+
+    wait("s", *st)
+    have = {n for (_, n) in waited}
+    wait("s", *[n for n in total if n not in have])

@@ -4,44 +4,41 @@ from concourse.mybir import dt, AluOpType, ActivationFunctionType
 F8 = "float8_e4m3fn_x4"
 CW, SLOT = 256, 32
 NO = CW // 16
-WS = 2
 LIFT, DROP = 4096.0, 1048576.0
+CODES, SCALES = 0, 1
 
 SCRATCH = {
+    "XB": ("sbuf", [128, 4096], "bfloat16"),
     "WB": ("sbuf", [128, 2048], "bfloat16"),
     "WQ": ("sbuf", [128, 512], F8), "WP": ("sbuf", [128, 512], "uint8"),
     "KA": ("sbuf", [128, CW], F8), "PA": ("sbuf", [128, CW], "uint8"),
-    "SLI": ("sbuf", [128, 48], "int32"), "PAI": ("sbuf", [128, 48], "int32"),
-    "OS": ("sbuf", [128, 48], "uint16"),
-    "OP": ("sbuf", [128, 48], "uint16"),
-    "pi": ("sbuf", [128, 2], "int32"), "pm": ("sbuf", [128, 2], "int32"), "pf": ("sbuf", [128, 2], "float32"),
-    "lf": ("sbuf", [128, 2], "float32"),
-    "J16": ("sbuf", [128, CW], "float32"), "mask": ("sbuf", [128, CW], "float32"), "step": ("sbuf", [128, CW], "float32"),
-    "BJ": ("sbuf", [128, 48], "int32"), "BJ2": ("sbuf", [128, 48], "int32"),
-    "neg": ("sbuf", [128, 48], "int32"), "new": ("sbuf", [128, 48], "int32"), "par": ("sbuf", [128, 48], "int32"),
-    "IW": ("sbuf", [128, 768], "float32"),
     "Z": ("sbuf", [128, 768], "float32"),
+    "SLI": ("sbuf", [128, 48], "int32"), "PAI": ("sbuf", [128, 48], "int32"),
+    "OS": ("sbuf", [128, 2 * NO], "uint16"),
+    "OP": ("sbuf", [128, 48], "uint16"),
+    "OPC": ("sbuf", [128, NO], "uint16"),
+    "CO": ("sbuf", [128, 2 * NO], "uint16"),
+    "pi": ("sbuf", [128, NO], "int32"), "pm": ("sbuf", [128, NO], "int32"), "pu": ("sbuf", [128, NO], "uint16"),
+    "pf": ("sbuf", [128, 2], "float32"), "lf": ("sbuf", [128, 2], "float32"),
+    "J16": ("sbuf", [128, 16], "float32"), "mask": ("sbuf", [128, 16], "float32"), "s16": ("sbuf", [128, 16], "float32"),
+    "step": ("sbuf", [128, CW], "float32"),
+    "BJ": ("sbuf", [128, 48], "int32"), "BJ2": ("sbuf", [128, 48], "int32"),
+    "low": ("sbuf", [128, 48], "int32"), "par": ("sbuf", [128, 48], "int32"),
+    "IW": ("sbuf", [128, 768], "float32"),
+    "RP": ("sbuf", [128, CW], "float32"), "CM": ("sbuf", [128, CW], "float32"), "SC": ("sbuf", [128, CW], "float32"),
+    "Y": ("sbuf", [128, 1024], "float32"),
 }
-for _t in range(4):
-    SCRATCH["X%d" % _t] = ("sbuf", [128, 1024], "bfloat16")
-    SCRATCH["Y%d" % _t] = ("sbuf", [128, 256], "float32")
 for _t in (1, 2, 3):
     SCRATCH["W%d" % _t] = ("sbuf", [128, 768], F8)
     SCRATCH["P%d" % _t] = ("sbuf", [128, 768], "uint8")
     SCRATCH["S%d" % _t] = ("sbuf", [128, CW], F8)
     SCRATCH["SS%d" % _t] = ("sbuf", [128, CW], "uint8")
-for _t in (2, 3):
-    SCRATCH["RP%d" % _t] = ("sbuf", [128, CW], "float32")
-    SCRATCH["CM%d" % _t] = ("sbuf", [128, CW], "float32")
-    SCRATCH["SC%d" % _t] = ("sbuf", [128, CW], "float32")
-    SCRATCH["CO%d" % _t] = ("sbuf", [128, NO], "uint16")
-for _t in range(7):
+for _t in range(8):
     SCRATCH["ps%d" % _t] = ("psum", [128, 512], "float32")
 
-SEMAPHORES = (["lsl", "lpa", "lwa", "lwb", "lx0", "lx1", "lx2", "lx3"]
-              + ["%s%d" % (n, t) for n in ("ac", "as") for t in (1, 2, 3)]
-              + ["%s%d%d" % (n, t, k) for n in ("lc", "ls") for t in (1, 2, 3) for k in range(3)]
-              + ["e%d" % i for i in range(100)])
+SEMAPHORES = (["lsl", "lpa", "lwa", "lwb", "lx0", "lx1", "lx2", "ap3", "ae3", "af3"]
+              + ["%s%d" % (n, t) for n in ("ac", "as", "lc", "ls", "le") for t in (1, 2, 3)]
+              + ["e%d" % i for i in range(120)])
 
 
 def plan(T, topo, src, t):
@@ -49,38 +46,33 @@ def plan(T, topo, src, t):
     for d in T.cores:
         if topo.chip(d) not in chips:
             chips.append(topo.chip(d))
-    n, own = len(chips), chips.index(topo.chip(src))
-    far = [[T.rank_of(d) for d in T.cores if topo.chip(d) == chips[(own + k) % n]] for k in (2, 1, 3)]
+    own = chips.index(topo.chip(src))
+    far = [[d for d in T.cores if topo.chip(d) == chips[own ^ k]] for k in ((2, 3, 1) if t < 3 else (1, 3, 2))]
+    for gr in far:
+        gr.sort(key=lambda d: topo.die(d) != topo.die(src))
     peer = [d for d in T.cores if d != src and topo.chip(d) == topo.chip(src)][0]
-    eng = topo.engines(src, T.cores[far[0][0]])
+    eng = topo.engines(src, far[0][0])
     even, odd = eng[0::2], eng[1::2]
     near = [e for e in topo.engines(src, peer) if e not in eng]
-    p = {T.rank_of(peer): [near[0], near[2]]}
+    far = [[T.rank_of(d) for d in gr] for gr in far]
+    p = {T.rank_of(peer): near[0::2]}
 
-    def one(gr):
+    def both(gr):
         return {gr[0]: even, gr[1]: odd}
 
-    def two(g1, g2):
-        m = len(even) // 2
-        return {g1[0]: even[:m], g1[1]: even[m:], g2[0]: odd[:m], g2[1]: odd[m:]}
-
-    steps = [far[0], far[1], far[2] + list(p)]
-    codes = [one(far[0]), one(far[1]), {**one(far[2]), **p}]
-    if t < 3:
-        scales = [one(far[0]), {**two(far[1], far[2]), **p}]
-    else:
-        scales = [two(far[0], far[1]), {**one(far[2]), **p}]
-    return steps, codes, scales
+    a, b = far[0] if t == 1 else far[0][::-1]
+    steps = codes = [{a: eng}, {b: eng}, both(far[1]), {**both(far[2][::-1]), **p}]
+    scales = steps[2:] + steps[:2]
+    if t == 3:
+        steps = steps[:3] + [both(far[2][::-1]), p]
+    calls = [(CODES, c) for c in codes] + [(SCALES, c) for c in scales]
+    return [(min(s), max(s) + 1) for s in steps], calls
 
 
-def runs(ranks, own):
-    out = []
-    for d in sorted(ranks):
-        if out and (d == out[-1][1] or (d == out[-1][1] + 1 and out[-1][1] == own)):
-            out[-1][1] = d + 1
-        else:
-            out.append([d, d + 1])
-    return out
+def arrival(t, part, s, d):
+    if t == 3 and part == SCALES:
+        return ("ap3", "as3", "ae3", "af3")[(s // 2) ^ (d // 2)]
+    return "a%s%d" % ("cs"[part], t)
 
 
 def bits(engines):
@@ -97,6 +89,7 @@ def rank_program(g, core, T, topo):
     qs = {"g": g, "v": g.vector, "a": g.scalar, "t": g.tensor, "s": g.sync}
     total, waited, count = {}, {}, [0]
     Copy, Ident = ActivationFunctionType.Copy, ActivationFunctionType.Identity
+    LO, HI = slice(0, 64), slice(64, 128)
 
     def wait(q, *names):
         for n in names:
@@ -104,182 +97,219 @@ def rank_program(g, core, T, topo):
                 qs[q].wait_ge(T.sem[n], total[n])
                 waited[(q, n)] = total[n]
 
+    def fresh():
+        count[0] += 1
+        return "e%d" % (count[0] - 1)
+
     def did(ins, n=1, name=None):
-        if name is None:
-            name = "e%d" % count[0]
-            count[0] += 1
+        name = name or fresh()
         ins.then_inc(T.sem[name], n)
         total[name] = total.get(name, 0) + n
         return name
 
-    def pickc(src, hi, off, dst, a, b, deps):
-        wait("v", *deps)
-        return did(g.vector.tensor_copy(dst[:, a:b].bitcast(dt.uint32), src[:, 0:hi].bitcast(dt.uint32).indirect(off)))
-
-    def picks(src, hi, off, dst, a, b, deps):
-        wait("a", *deps)
-        return did(g.scalar.activation(dst[:, a:b], src[:, 0:hi].indirect(off), Copy))
+    def pick(q, part, src, off, dst, deps):
+        wait(q, *deps)
+        if part == CODES:
+            return did(g.vector.tensor_copy(dst.bitcast(dt.uint32), src.bitcast(dt.uint32).indirect(off)))
+        if q == "v":
+            return did(g.vector.tensor_copy(dst, src.indirect(off)))
+        return did(g.scalar.activation(dst, src.indirect(off), Copy))
 
     def dma(q, dst, src, name=None, after=()):
         wait(q, *after)
         return did(qs[q].dma_start(dst, src), 16, name)
 
-    mine = {t: plan(T, topo, core, t) for t in (1, 2, 3)}
+    def halves(dst, lo, hi, deps):
+        name = fresh()
+        wait("v", *deps)
+        did(g.vector.tensor_copy(dst[LO, :], lo), 1, name)
+        return did(g.vector.tensor_copy(dst[HI, :], hi), 1, name)
+
     for t in (1, 2, 3):
-        for arr, loc, part in (("ac", "lc", 1), ("as", "ls", 2)):
-            total["%s%d" % (arr, t)] = sum(len(c[r]) for s in T.cores if s != core
-                                           for c in plan(T, topo, s, t)[part] if r in c)
-            for k, c in enumerate(mine[t][part]):
-                total["%s%d%d" % (loc, t, k)] = sum(len(e) for e in c.values())
+        for s in T.cores:
+            for part, c in plan(T, topo, s, t)[1]:
+                if r in c:
+                    name = arrival(t, part, T.rank_of(s), r)
+                    total[name] = total.get(name, 0) + len(c[r])
     at = CW + SLOT * r
 
-    def exchange(t, part, win, hi, off, deps):
-        pick, dst, land, arr, loc = ((pickc, T["S%d" % t], T["W%d" % t], "ac", "lc"),
-                                     (picks, T["SS%d" % t], T["P%d" % t], "as", "ls"))[part]
-        for k, c in enumerate(mine[t][part + 1]):
-            ready = []
-            for st in mine[t][0]:
-                if st[0] in c:
-                    for a, b in runs(st, r):
-                        ready.append(pick(win, hi, off[:, 2 * a:2 * b], dst, SLOT * a, SLOT * b, deps))
-            trs = []
+    def exchange(t, wins, off, o, deps, then={}):
+        pieces, calls = plan(T, topo, core, t)
+        done = {}
+        for n, (part, c) in enumerate(calls):
+            dst, land = T[("S%d", "SS%d")[part] % t], T["%s%d" % ("WP"[part], t)]
+            ready, trs = [], []
+            for i, (a, b) in enumerate(pieces):
+                if any(a <= d < b for d in c):
+                    if (part, a) not in done:
+                        done[(part, a)] = pick("va"[part], part, wins[part], off[:, o + 2 * a:o + 2 * b],
+                                               dst[:, SLOT * a:SLOT * b], deps[part])
+                        if (part, i) in then:
+                            then[(part, i)]()
+                    ready.append(done[(part, a)])
             for d, e in c.items():
                 rid, pid, _ = topo.addr(T.cores[d])
                 s, w = dst[:, SLOT * d:SLOT * d + SLOT], land[:, at:at + SLOT]
-                if part == 0:
+                if part == CODES:
                     s, w = s.bitcast(dt.uint8), w.bitcast(dt.uint8)
                 trs.append(RemoteDMATransfer(dst_ids=[DstId(rid=rid, pnc=pid)], dma_engine_mask=bits(e),
-                                             remote_sem=T.sem["%s%d" % (arr, t)], src=s, dst=w))
+                                             remote_sem=T.sem[arrival(t, part, r, d)], src=s, dst=w))
             wait("g", *ready)
-            g.remote_dma_fused(trs, local_sem=T.sem["%s%d%d" % (loc, t, k)])
+            left = "l%s%d" % ("e" if n == len(calls) - (4 if t < 3 else 2) else "cs"[part], t)
+            if len(trs) == 1:
+                g.remote_dma(w, s, T.sem[arrival(t, part, r, d)], T.sem[left], pid, rid, bits(e))
+            else:
+                g.remote_dma_fused(trs, local_sem=T.sem[left])
+            total[left] = total.get(left, 0) + sum(len(e) for e in c.values())
 
-    dma("s", T.X0[:, :], T.x[:, 0:1024], "lx0")
-    for i in range(8):
-        dma("a" if i < 4 else "s", T.SLI[16 * i:16 * i + 16, :], T.sl[:, :], "lsl")
-    for i in range(8):
-        dma("a" if i < 2 else "s", T.PAI[16 * i:16 * i + 16, :], T.pa[:, :], "lpa")
-    dma("s", T.X1[:, :], T.x[:, 1024:2048], "lx1")
-    dma("s", T.X2[:, :], T.x[:, 2048:3072], "lx2")
-    dma("s", T.X3[:, :], T.x[:, 3072:4096], "lx3", ["lx0"])
+    def piece(t):
+        return T.XB[:, 1024 * t:1024 * t + 1024]
 
-    i_pi = did(g.iota(T.pi[:, 0:1], [[0, 1]], 0, 1))
-    i_w = did(g.iota(T.IW[:, 0:256], [[1, 256]], 0, 0, allow_small_or_imprecise_dtypes=True))
+    def product(ps, wt, win, pl, deps):
+        wait("t", *deps)
+        return did(g.tensor.matmul_mx(ps, T.WQ[:, 128 * wt:128 * wt + 128], T.WP[:, 128 * wt:128 * wt + 128], win, pl, True, True))
+
+    xa = dma("s", T.XB[:, 0:512], T.x[:, 0:512])
+    dma("a", T.XB[:, 512:1024], T.x[:, 512:1024], "lx0")
+    for i in range(8):
+        dma("as"[i % 2], T.SLI[16 * i:16 * i + 16, :], T.sl[:, :], "lsl")
+    for i in range(4):
+        dma("as"[i % 2], T.PAI[16 * i:16 * i + 16, :], T.pa[:, :], "lpa")
+    dma("s", piece(1), T.x[:, 1024:2048], "lx1")
+
+    i_pi = did(g.iota(T.pi[:, :], [[0, NO]], 0, 1))
+    i_j16 = did(g.iota(T.J16[:, :], [[1, 16]], 0, 0, allow_small_or_imprecise_dtypes=True))
     i_b = did(g.iota(T.BJ[:, :], [[0, 3], [16, 16]], 512, 0))
-    i_j16 = did(g.iota(T.J16[:, :], [[0, NO], [1, 16]], 0, 0, allow_small_or_imprecise_dtypes=True))
+    i_w = did(g.iota(T.IW[:, 0:256], [[1, 256]], 0, 0, allow_small_or_imprecise_dtypes=True))
+    wait("v", i_pi)
+    v_pm = did(g.vector.tensor_scalar(T.pm[:, :], T.pi[:, :], 15, None, AluOpType.bitwise_and))
+    wait("v", v_pm)
+    v_pf = did(g.vector.tensor_copy(T.pf[:, 0:1], T.pm[:, 0:1]))
+    v_pu = did(g.vector.tensor_copy(T.pu[:, :], T.pm[:, :]))
+    wait("v", i_j16, v_pf)
+    v_mask = did(g.vector.tensor_scalar(T.mask[:, :], T.J16[:, :], T.pf[:, 0:1], -DROP, AluOpType.is_equal, AluOpType.mult))
+    v_lf = did(g.vector.tensor_scalar(T.lf[:, 0:1], T.pm[:, 0:1], -LIFT, 15 * LIFT, AluOpType.mult, AluOpType.add))
+    wait("v", v_mask)
+    v_s16 = did(g.vector.tensor_scalar(T.s16[:, :], T.mask[:, :], LIFT, None, AluOpType.add))
+    dma("s", T.XB[:, 2048:4096], T.x[:, 2048:4096], "lx2", [v_s16])
+    dma("s", T.WB[:, 0:1024], T.w[:, 0:1024], "lwa")
+    wait("a", v_s16, v_pu)
+    a_step = did(g.scalar.activation(T.step[:, :], T.s16[:, :].indirect(T.pu[:, :]), Copy))
     wait("a", i_w)
     i_w1 = did(g.scalar.activation(T.IW[:, 256:512], T.IW[:, 0:256], Ident, bias=256.0))
     i_w2 = did(g.scalar.activation(T.IW[:, 512:768], T.IW[:, 0:256], Ident, bias=512.0))
-    wait("v", i_pi)
-    v_pm = did(g.vector.tensor_scalar(T.pm[:, 0:1], T.pi[:, 0:1], 15, None, AluOpType.bitwise_and))
-    wait("v", v_pm)
-    v_pf = did(g.vector.tensor_copy(T.pf[:, 0:1], T.pm[:, 0:1]))
-    v_lf = did(g.vector.tensor_scalar(T.lf[:, 0:1], T.pm[:, 0:1], -LIFT, 15 * LIFT, AluOpType.mult, AluOpType.add))
-    wait("v", i_b, v_pf)
-    n0 = did(g.vector.tensor_scalar(T.BJ2[:, :], T.BJ[:, :], T.pf[:, 0:1], None, AluOpType.add))
+    wait("v", i_b)
+    n0 = did(g.vector.tensor_scalar(T.BJ2[LO, :], T.BJ[LO, :], T.pf[LO, 0:1], None, AluOpType.add))
 
+    n2, cm, made = fresh(), fresh(), {}
+
+    def parents():
+        wait("v", "lpa")
+        n1 = did(g.vector.tensor_scalar(T.low[LO, :], T.PAI[LO, :], 1023, None, AluOpType.bitwise_and))
+        wait("v", n0, n1)
+        did(g.vector.tensor_tensor(T.par[LO, :], T.low[LO, :], T.BJ2[LO, :], AluOpType.min), 1, n2)
+        made["opc"] = halves(T.OPC, T.par[LO, 0:16], T.par[LO, 16:32], [n2])
+
+    def later_slots():
+        made["osc"] = halves(T.OS[:, 16:32], T.SLI[LO, 16:32], T.SLI[HI, 32:48], [])
+
+    def compose():
+        wait("a", made["opc"], i_w1, i_w2)
+        rp = did(g.scalar.activation(T.RP[:, :], T.IW[:, :].indirect(T.OPC[:, :]), Copy))
+        wait("a", rp, made["osc"])
+        did(g.scalar.activation(T.CM[:, :], T.RP[:, :].indirect(T.OS[:, 16:32]), Copy), 1, cm)
+
+    k0 = fresh()
+    wait("v", xa)
+    did(g.vector.quantize_mx(T.KA[:, 0:128], T.PA[:, 0:128], T.XB[:, 0:512]), 1, k0)
     wait("v", "lx0")
-    k0 = did(g.vector.quantize_mx(T.KA[:, :], T.PA[:, :], T.X0[:, :]))
+    did(g.vector.quantize_mx(T.KA[:, 128:256], T.PA[:, 128:256], T.XB[:, 512:1024]), 1, k0)
     wait("v", "lsl")
-    os_ = did(g.vector.tensor_copy(T.OS[:, :], T.SLI[:, :]))
-    exchange(1, 0, T.KA, CW, T.OS[:, 0:NO], [os_, k0])
-    exchange(1, 1, T.PA, CW, T.OS[:, 0:NO], [os_, k0])
+    os_ = did(g.vector.tensor_copy(T.OS[:, 0:16], T.SLI[:, 0:16]))
+    exchange(1, (T.KA[:, :], T.PA[:, :]), T.OS, 0, ([os_, k0], [os_, k0]),
+             {(CODES, 1): parents, (CODES, 3): later_slots, (SCALES, 1): compose})
 
-    wait("v", "lpa")
-    n1 = did(g.vector.tensor_scalar(T.neg[:, :], T.PAI[:, :], 0, None, AluOpType.is_lt))
-    wait("v", n0, n1)
-    n2 = did(g.vector.tensor_tensor(T.new[:, :], T.neg[:, :], T.BJ2[:, :], AluOpType.mult))
-    wait("v", n2)
-    n3 = did(g.vector.tensor_tensor(T.par[:, :], T.new[:, :], T.PAI[:, :], AluOpType.max))
-    wait("v", n3)
-    pa = did(g.vector.tensor_copy(T.OP[:, :], T.par[:, :]))
-    wait("v", i_j16)
-    v_mask = did(g.vector.tensor_scalar(T.mask[:, :], T.J16[:, :], T.pf[:, 0:1], -DROP, AluOpType.is_equal, AluOpType.mult))
-    wait("v", v_mask)
-    v_step = did(g.vector.tensor_scalar(T.step[:, :], T.mask[:, :], LIFT, None, AluOpType.add))
-    q0 = did(g.vector.quantize_mx(T.W1[:, 0:256], T.P1[:, 0:256], T.X0[:, :]))
+    q0 = did(g.vector.quantize_mx(T.W1[:, 0:256], T.P1[:, 0:256], piece(0)))
     wait("v", "lx1")
-    x1 = did(g.vector.quantize_mx(T.W1[:, 512:768], T.P1[:, 512:768], T.X1[:, :]))
+    x1 = did(g.vector.quantize_mx(T.W1[:, 512:768], T.P1[:, 512:768], piece(1)))
+    wait("v", cm, a_step)
+    sc = did(g.vector.tensor_tensor_scan(T.SC[:, :], T.step[:, :], T.CM[:, :], 0.0, AluOpType.add, AluOpType.max))
 
-    def compose_a(t):
-        wait("a", pa, os_, i_w, i_w1, i_w2)
-        e = did(g.scalar.activation(T["RP%d" % t][:, :], T.IW[:, 0:768].indirect(T.OP[:, 16 * (t - 2):16 * (t - 1)]), Copy))
-        wait("a", e)
-        return did(g.scalar.activation(T["CM%d" % t][:, :], T["RP%d" % t][:, :].indirect(T.OS[:, NO * (t - 1):NO * t]), Copy))
+    def offsets(i, half):
+        name = fresh()
+        wait("v", sc, v_lf)
+        for to in (LO, HI):
+            did(g.vector.tensor_scalar(T.CO[to, NO * i:NO * i + NO], T.SC[half, 15:CW:16], T.lf[half, 0:1], None, AluOpType.subtract), 1, name)
+        return name
 
-    def compose_v(t, e):
-        wait("v", e, v_step)
-        b = did(g.vector.tensor_tensor_scan(T["SC%d" % t][:, :], T.step[:, :], T["CM%d" % t][:, :], 0.0,
-                                            AluOpType.add, AluOpType.max))
-        wait("v", b, v_lf)
-        return did(g.vector.tensor_scalar(T["CO%d" % t][:, :], T["SC%d" % t][:, 15:CW:16], T.lf[:, 0:1], None, AluOpType.subtract))
-
-    co2 = compose_v(2, compose_a(2))
-    ca3 = compose_a(3)
-    own = T.OS[:, 2 * r:2 * r + 2]
-    fc = pickc(T.KA, CW, own, T.W3, at, at + SLOT, [os_, k0])
-    fs = picks(T.PA, CW, own, T.P3, at, at + SLOT, [os_, k0])
-    dma("s", T.WB[:, 0:512 * WS], T.w[:, 0:512 * WS], "lwa", ["lc12"])
+    co2 = offsets(0, LO)
+    dma("s", T.WB[:, 1536:2048], T.w[:, 1536:2048], "lwb", ["le1"])
 
     d = [q0, x1, co2]
-    exchange(2, 0, T.W1, 768, T.CO2, d + ["ac1"])
-    exchange(2, 1, T.P1, 768, T.CO2, d + ["as1"])
 
-    k1c = pickc(T.W1, 768, T.OP[:, 0:16], T.W2, 0, CW, [pa, "ac1", q0, x1])
-    wait("v", "lx2")
-    x2 = did(g.vector.quantize_mx(T.W2[:, 512:768], T.P2[:, 512:768], T.X2[:, :]))
-    co3 = compose_v(3, ca3)
-    k1s = picks(T.P1, 768, T.OP[:, 0:16], T.P2, 0, CW, [pa, "as1", q0, x1])
-    dma("s", T.WB[:, 512 * WS:2048], T.w[:, 512 * WS:2048], "lwb", ["lc20"])
+    def later_lists():
+        made["pa"] = halves(T.OP, T.par[LO, :], T.par[LO, :], [n2])
+        made["co3"] = offsets(1, HI)
 
-    exchange(3, 0, T.W2, 768, T.CO3, [k1c, x2, co3, "ac2"])
-    exchange(3, 1, T.P2, 768, T.CO3, [k1s, x2, co3, "as2"])
+    exchange(2, (T.W1[:, :], T.P1[:, :]), T.CO, 0, (d + ["ac1"], d + ["as1"]), {(CODES, 3): later_lists})
 
-    k2c = pickc(T.W2, 768, T.OP[:, 16:32], T.W3, 0, CW, [pa, "ac2", k1c, x2])
-    k2s = picks(T.P2, 768, T.OP[:, 16:32], T.P3, 0, CW, [pa, "as2", k1s, x2])
+    lwc = dma("s", T.WB[:, 1024:1536], T.w[:, 1024:1536], None, ["le2"])
+    pa, co3 = made["pa"], made["co3"]
+    k1c = pick("v", CODES, T.W1[:, :], T.OP[:, 0:16], T.W2[:, 0:CW], [pa])
     wait("v", "lwa")
-    wqa = did(g.vector.quantize_mx(T.WQ[:, 0:128 * WS], T.WP[:, 0:128 * WS], T.WB[:, 0:512 * WS]))
-    wait("v", "lx3")
-    x3 = did(g.vector.quantize_mx(T.W3[:, 512:768], T.P3[:, 512:768], T.X3[:, :]))
-    wait("v", "lwb")
-    wqb = did(g.vector.quantize_mx(T.WQ[:, 128 * WS:512], T.WP[:, 128 * WS:512], T.WB[:, 512 * WS:2048]))
-
-    def product(ps, wt, win, pl, a, b, deps):
-        wait("t", wqa if wt < WS else wqb, *deps)
-        return did(g.tensor.matmul_mx(T["ps%d" % ps][:, 0:b - a], T.WQ[:, 128 * wt:128 * wt + 128], T.WP[:, 128 * wt:128 * wt + 128],
-                                      win[:, a:b], pl[:, a:b], True, True))
-
-    m0 = product(0, 0, T.W1, T.P1, 0, 256, [q0])
-    m1 = product(1, 1, T.W2, T.P2, 0, 256, [k1c, k1s])
-    mo = product(3, 3, T.W3, T.P3, 0, 256, [k2c, k2s])
-    mn = product(4, 3, T.W3, T.P3, 512, 768, [x3])
-    m2 = product(2, 2, T.W3, T.P3, 0, 256, [k2c, k2s])
+    wqa = did(g.vector.quantize_mx(T.WQ[:, 0:256], T.WP[:, 0:256], T.WB[:, 0:1024]))
+    wait("v", "lx2")
+    x2 = did(g.vector.quantize_mx(T.W2[:, 512:768], T.P2[:, 512:768], piece(2)))
+    k1s = pick("a", SCALES, T.P1[:, :], T.OP[:, 0:16], T.P2[:, 0:CW], [pa])
+    own = T.OS[:, 2 * r:2 * r + 2]
+    fs = pick("a", SCALES, T.PA[:, :], own, T.P3[:, at:at + SLOT], [])
+    m0 = product(T.ps0[:, 0:CW], 0, T.W1[:, 0:CW], T.P1[:, 0:CW], [wqa, q0])
+    m1 = product(T.ps1[:, 0:CW], 1, T.W2[:, 0:CW], T.P2[:, 0:CW], [k1c, k1s])
     wait("a", m0)
-    y0 = did(g.scalar.activation(T.Y0[:, :], T.ps0[:, 0:256], Copy))
-    wait("v", m1)
-    y1 = did(g.vector.tensor_copy(T.Y1[:, :], T.ps1[:, 0:256]))
-    wait("a", mo)
-    zo = did(g.scalar.activation(T.Z[:, 0:256], T.ps3[:, 0:256], Copy))
+    y0 = did(g.scalar.activation(T.Y[:, 0:256], T.ps0[:, 0:256], Copy))
+    wait("a", m1)
+    y1 = did(g.scalar.activation(T.Y[:, 256:512], T.ps1[:, 0:256], Copy))
+
+    exchange(3, (T.W2[:, :], T.P2[:, :]), T.CO, NO, ([k1c, x2, co3, "ac2"], [k1s, x2, co3, "as2"]))
+
+    k2c = pick("v", CODES, T.W2[:, :], T.OP[:, 16:32], T.W3[:, 0:CW], [])
+    k2s = pick("a", SCALES, T.P2[:, :], T.OP[:, 16:32], T.P3[:, 0:CW], [])
+    x3 = did(g.vector.quantize_mx(T.W3[:, 512:768], T.P3[:, 512:768], piece(3)))
+    wait("v", "lwb")
+    wait("v", lwc)
+    wqb = did(g.vector.quantize_mx(T.WQ[:, 256:512], T.WP[:, 256:512], T.WB[:, 1024:2048]))
+    mn = product(T.ps5[:, 0:CW], 3, T.W3[:, 512:768], T.P3[:, 512:768], [wqb, x3])
+    mo = product(T.ps6[:, 0:CW], 3, T.W3[:, 0:CW], T.P3[:, 0:CW], [k2c, k2s])
+    m2 = product(T.ps2[:, 0:CW], 2, T.W3[:, 0:CW], T.P3[:, 0:CW], [])
+    fc = pick("v", CODES, T.KA[:, :], own, T.W3[:, at:at + SLOT], [])
     wait("v", mn)
-    zn = did(g.vector.tensor_copy(T.Z[:, 512:768], T.ps4[:, 0:256]))
-    wait("a", m2)
-    y2 = did(g.scalar.activation(T.Y2[:, :], T.ps2[:, 0:256], Copy))
-    st = [dma("s", T.y[:, 0:256], T.Y0[:, :], None, [y0, "lc32"]),
-          dma("s", T.y[:, 256:512], T.Y1[:, :], None, [y1]),
-          dma("s", T.y[:, 512:768], T.Y2[:, :], None, [y2])]
+    zn = did(g.vector.tensor_copy(T.Z[:, 512:768], T.ps5[:, 0:256]))
+    wait("a", mo)
+    zo = did(g.scalar.activation(T.Z[:, 0:256], T.ps6[:, 0:256], Copy))
+    wait("v", m2)
+    y2 = did(g.vector.tensor_copy(T.Y[:, 512:768], T.ps2[:, 0:256]))
+    st = [dma("s", T.y[:, 0:768], T.Y[:, 0:768], None, [y0, y1, y2, "le3"])]
 
-    ma = product(5, 3, T.W3, T.P3, 256, 384, ["ac3", "as3", fc, fs])
-    mb = product(6, 3, T.W3, T.P3, 384, 512, ["ac3", "as3", fc, fs])
-    wait("a", ma)
-    za = did(g.scalar.activation(T.Z[:, 256:384], T.ps5[:, 0:128], Copy))
-    wait("v", mb)
-    zb = did(g.vector.tensor_copy(T.Z[:, 384:512], T.ps6[:, 0:128]))
-    wait("v", pa, zo, zn, za, zb)
-    fa = did(g.vector.tensor_copy(T.Y3[:, 0:128], T.Z[:, 0:768].indirect(T.OP[:, 32:40])))
-    wait("a", pa, zo, zn, za, zb)
-    fb = did(g.scalar.activation(T.Y3[:, 128:256], T.Z[:, 0:768].indirect(T.OP[:, 40:48]), Copy))
-    st.append(dma("s", T.y[:, 768:896], T.Y3[:, 0:128], None, [fa]))
-    st.append(dma("a", T.y[:, 896:1024], T.Y3[:, 128:256], None, [fb]))
+    def slots(q, ps, a, b, n, deps):
+        m = product(ps[:, 0:128], 3, T.W3[:, a:a + 128], T.P3[:, a:a + 128], deps)
+        wait(q, m)
+        if q == "v":
+            return did(g.vector.tensor_copy(T.Z[:, b:b + n], ps[:, b - a:b - a + n]))
+        return did(g.scalar.activation(T.Z[:, b:b + n], ps[:, b - a:b - a + n], Copy))
 
-    wait("s", *st)
+    home, other = CW + 64 * (r // 2), CW + 128 * (1 - r // 4)
+    late = CW + 64 * ((r // 2) ^ 1)
+    zh = slots("v", T.ps7, home - 64 if late > home else home, home, 64, [fc, fs, "ac3", "af3", "ap3"])
+    za = slots("a", T.ps3, other, other, 128, ["ae3"])
+    zb = slots("v", T.ps4, min(home, late), late, 64, ["as3"])
+    wait("v", zo, zn, za, zh, zb)
+    wait("a", zo, zn, za, zh, zb)
+    for a in (768, 896):
+        o = 32 + (a - 768) // 16
+        ya = did(g.vector.tensor_copy(T.Y[:, a:a + 64], T.Z[:, :].indirect(T.OP[:, o:o + 4])))
+        yb = did(g.scalar.activation(T.Y[:, a + 64:a + 128], T.Z[:, :].indirect(T.OP[:, o + 4:o + 8]), Copy))
+        st.append(dma("s", T.y[:, a:a + 128], T.Y[:, a:a + 128], None, [ya, yb]))
+
     have = {n for (_, n) in waited}
-    wait("s", *[n for n in total if n not in have])
+    wait("g", *[n for n in total if n not in have and n not in st])
+    wait("s", *st)

from concourse.bass import DstId, RemoteDMATransfer
from concourse.mybir import dt, AluOpType, ActivationFunctionType

F8 = "float8_e4m3fn_x4"
CW, SLOT = 256, 32
NO = CW // 16
LIFT, DROP = 4096.0, 1048576.0
CODES, SCALES = 0, 1

SCRATCH = {
    "XB": ("sbuf", [128, 4096], "bfloat16"),
    "WB": ("sbuf", [128, 2048], "bfloat16"),
    "WQ": ("sbuf", [128, 512], F8), "WP": ("sbuf", [128, 512], "uint8"),
    "KA": ("sbuf", [128, CW], F8), "PA": ("sbuf", [128, CW], "uint8"),
    "Z": ("sbuf", [128, 768], "float32"),
    "SLI": ("sbuf", [128, 48], "int32"), "PAI": ("sbuf", [128, 48], "int32"),
    "OS": ("sbuf", [128, 2 * NO], "uint16"),
    "OP": ("sbuf", [128, 48], "uint16"),
    "OPC": ("sbuf", [128, NO], "uint16"),
    "CO": ("sbuf", [128, 2 * NO], "uint16"),
    "pi": ("sbuf", [128, NO], "int32"), "pm": ("sbuf", [128, NO], "int32"), "pu": ("sbuf", [128, NO], "uint16"),
    "pf": ("sbuf", [128, 2], "float32"), "lf": ("sbuf", [128, 2], "float32"),
    "J16": ("sbuf", [128, 16], "float32"), "mask": ("sbuf", [128, 16], "float32"), "s16": ("sbuf", [128, 16], "float32"),
    "step": ("sbuf", [128, CW], "float32"),
    "BJ": ("sbuf", [128, 48], "int32"), "BJ2": ("sbuf", [128, 48], "int32"),
    "low": ("sbuf", [128, 48], "int32"), "par": ("sbuf", [128, 48], "int32"),
    "IW": ("sbuf", [128, 768], "float32"),
    "RP": ("sbuf", [128, CW], "float32"), "CM": ("sbuf", [128, CW], "float32"), "SC": ("sbuf", [128, CW], "float32"),
    "Y": ("sbuf", [128, 1024], "float32"),
}
for _t in (1, 2, 3):
    SCRATCH["W%d" % _t] = ("sbuf", [128, 768], F8)
    SCRATCH["P%d" % _t] = ("sbuf", [128, 768], "uint8")
    SCRATCH["S%d" % _t] = ("sbuf", [128, CW], F8)
    SCRATCH["SS%d" % _t] = ("sbuf", [128, CW], "uint8")
for _t in range(8):
    SCRATCH["ps%d" % _t] = ("psum", [128, 512], "float32")

SEMAPHORES = (["lsl", "lpa", "lwa", "lwb", "lx0", "lx1", "lx2", "ap3", "ae3", "af3"]
              + ["%s%d" % (n, t) for n in ("ac", "as", "lc", "ls", "le") for t in (1, 2, 3)]
              + ["e%d" % i for i in range(120)])


def plan(T, topo, src, t):
    chips = []
    for d in T.cores:
        if topo.chip(d) not in chips:
            chips.append(topo.chip(d))
    own = chips.index(topo.chip(src))
    far = [[d for d in T.cores if topo.chip(d) == chips[own ^ k]] for k in ((2, 3, 1) if t < 3 else (1, 3, 2))]
    for gr in far:
        gr.sort(key=lambda d: topo.die(d) != topo.die(src))
    peer = [d for d in T.cores if d != src and topo.chip(d) == topo.chip(src)][0]
    eng = topo.engines(src, far[0][0])
    even, odd = eng[0::2], eng[1::2]
    near = [e for e in topo.engines(src, peer) if e not in eng]
    far = [[T.rank_of(d) for d in gr] for gr in far]
    p = {T.rank_of(peer): near[0::2]}

    def both(gr):
        return {gr[0]: even, gr[1]: odd}

    a, b = far[0] if t == 1 else far[0][::-1]
    steps = codes = [{a: eng}, {b: eng}, both(far[1]), {**both(far[2][::-1]), **p}]
    scales = steps[2:] + steps[:2]
    if t == 3:
        steps = steps[:3] + [both(far[2][::-1]), p]
    calls = [(CODES, c) for c in codes] + [(SCALES, c) for c in scales]
    return [(min(s), max(s) + 1) for s in steps], calls


def arrival(t, part, s, d):
    if t == 3 and part == SCALES:
        return ("ap3", "as3", "ae3", "af3")[(s // 2) ^ (d // 2)]
    return "a%s%d" % ("cs"[part], t)


def bits(engines):
    m = 0
    for e in engines:
        m |= 1 << e
    return m


def rank_program(g, core, T, topo):
    r = T.rank_of(core)
    if r is None:
        return
    qs = {"g": g, "v": g.vector, "a": g.scalar, "t": g.tensor, "s": g.sync}
    total, waited, count = {}, {}, [0]
    Copy, Ident = ActivationFunctionType.Copy, ActivationFunctionType.Identity
    LO, HI = slice(0, 64), slice(64, 128)

    def wait(q, *names):
        for n in names:
            if waited.get((q, n)) != total[n]:
                qs[q].wait_ge(T.sem[n], total[n])
                waited[(q, n)] = total[n]

    def fresh():
        count[0] += 1
        return "e%d" % (count[0] - 1)

    def did(ins, n=1, name=None):
        name = name or fresh()
        ins.then_inc(T.sem[name], n)
        total[name] = total.get(name, 0) + n
        return name

    def pick(q, part, src, off, dst, deps):
        wait(q, *deps)
        if part == CODES:
            return did(g.vector.tensor_copy(dst.bitcast(dt.uint32), src.bitcast(dt.uint32).indirect(off)))
        if q == "v":
            return did(g.vector.tensor_copy(dst, src.indirect(off)))
        return did(g.scalar.activation(dst, src.indirect(off), Copy))

    def dma(q, dst, src, name=None, after=()):
        wait(q, *after)
        return did(qs[q].dma_start(dst, src), 16, name)

    def halves(dst, lo, hi, deps):
        name = fresh()
        wait("v", *deps)
        did(g.vector.tensor_copy(dst[LO, :], lo), 1, name)
        return did(g.vector.tensor_copy(dst[HI, :], hi), 1, name)

    for t in (1, 2, 3):
        for s in T.cores:
            for part, c in plan(T, topo, s, t)[1]:
                if r in c:
                    name = arrival(t, part, T.rank_of(s), r)
                    total[name] = total.get(name, 0) + len(c[r])
    at = CW + SLOT * r

    def exchange(t, wins, off, o, deps, then={}):
        pieces, calls = plan(T, topo, core, t)
        done = {}
        for n, (part, c) in enumerate(calls):
            dst, land = T[("S%d", "SS%d")[part] % t], T["%s%d" % ("WP"[part], t)]
            ready, trs = [], []
            for i, (a, b) in enumerate(pieces):
                if any(a <= d < b for d in c):
                    if (part, a) not in done:
                        done[(part, a)] = pick("va"[part], part, wins[part], off[:, o + 2 * a:o + 2 * b],
                                               dst[:, SLOT * a:SLOT * b], deps[part])
                        if (part, i) in then:
                            then[(part, i)]()
                    ready.append(done[(part, a)])
            for d, e in c.items():
                rid, pid, _ = topo.addr(T.cores[d])
                s, w = dst[:, SLOT * d:SLOT * d + SLOT], land[:, at:at + SLOT]
                if part == CODES:
                    s, w = s.bitcast(dt.uint8), w.bitcast(dt.uint8)
                trs.append(RemoteDMATransfer(dst_ids=[DstId(rid=rid, pnc=pid)], dma_engine_mask=bits(e),
                                             remote_sem=T.sem[arrival(t, part, r, d)], src=s, dst=w))
            wait("g", *ready)
            left = "l%s%d" % ("e" if n == len(calls) - (4 if t < 3 else 2) else "cs"[part], t)
            if len(trs) == 1:
                g.remote_dma(w, s, T.sem[arrival(t, part, r, d)], T.sem[left], pid, rid, bits(e))
            else:
                g.remote_dma_fused(trs, local_sem=T.sem[left])
            total[left] = total.get(left, 0) + sum(len(e) for e in c.values())

    def piece(t):
        return T.XB[:, 1024 * t:1024 * t + 1024]

    def product(ps, wt, win, pl, deps):
        wait("t", *deps)
        return did(g.tensor.matmul_mx(ps, T.WQ[:, 128 * wt:128 * wt + 128], T.WP[:, 128 * wt:128 * wt + 128], win, pl, True, True))

    xa = dma("s", T.XB[:, 0:512], T.x[:, 0:512])
    dma("a", T.XB[:, 512:1024], T.x[:, 512:1024], "lx0")
    for i in range(8):
        dma("as"[i % 2], T.SLI[16 * i:16 * i + 16, :], T.sl[:, :], "lsl")
    for i in range(4):
        dma("as"[i % 2], T.PAI[16 * i:16 * i + 16, :], T.pa[:, :], "lpa")
    dma("s", piece(1), T.x[:, 1024:2048], "lx1")

    i_pi = did(g.iota(T.pi[:, :], [[0, NO]], 0, 1))
    i_j16 = did(g.iota(T.J16[:, :], [[1, 16]], 0, 0, allow_small_or_imprecise_dtypes=True))
    i_b = did(g.iota(T.BJ[:, :], [[0, 3], [16, 16]], 512, 0))
    i_w = did(g.iota(T.IW[:, 0:256], [[1, 256]], 0, 0, allow_small_or_imprecise_dtypes=True))
    wait("v", i_pi)
    v_pm = did(g.vector.tensor_scalar(T.pm[:, :], T.pi[:, :], 15, None, AluOpType.bitwise_and))
    wait("v", v_pm)
    v_pf = did(g.vector.tensor_copy(T.pf[:, 0:1], T.pm[:, 0:1]))
    v_pu = did(g.vector.tensor_copy(T.pu[:, :], T.pm[:, :]))
    wait("v", i_j16, v_pf)
    v_mask = did(g.vector.tensor_scalar(T.mask[:, :], T.J16[:, :], T.pf[:, 0:1], -DROP, AluOpType.is_equal, AluOpType.mult))
    v_lf = did(g.vector.tensor_scalar(T.lf[:, 0:1], T.pm[:, 0:1], -LIFT, 15 * LIFT, AluOpType.mult, AluOpType.add))
    wait("v", v_mask)
    v_s16 = did(g.vector.tensor_scalar(T.s16[:, :], T.mask[:, :], LIFT, None, AluOpType.add))
    dma("s", T.XB[:, 2048:4096], T.x[:, 2048:4096], "lx2", [v_s16])
    dma("s", T.WB[:, 0:1024], T.w[:, 0:1024], "lwa")
    wait("a", v_s16, v_pu)
    a_step = did(g.scalar.activation(T.step[:, :], T.s16[:, :].indirect(T.pu[:, :]), Copy))
    wait("a", i_w)
    i_w1 = did(g.scalar.activation(T.IW[:, 256:512], T.IW[:, 0:256], Ident, bias=256.0))
    i_w2 = did(g.scalar.activation(T.IW[:, 512:768], T.IW[:, 0:256], Ident, bias=512.0))
    wait("v", i_b)
    n0 = did(g.vector.tensor_scalar(T.BJ2[LO, :], T.BJ[LO, :], T.pf[LO, 0:1], None, AluOpType.add))

    n2, cm, made = fresh(), fresh(), {}

    def parents():
        wait("v", "lpa")
        n1 = did(g.vector.tensor_scalar(T.low[LO, :], T.PAI[LO, :], 1023, None, AluOpType.bitwise_and))
        wait("v", n0, n1)
        did(g.vector.tensor_tensor(T.par[LO, :], T.low[LO, :], T.BJ2[LO, :], AluOpType.min), 1, n2)
        made["opc"] = halves(T.OPC, T.par[LO, 0:16], T.par[LO, 16:32], [n2])

    def later_slots():
        made["osc"] = halves(T.OS[:, 16:32], T.SLI[LO, 16:32], T.SLI[HI, 32:48], [])

    def compose():
        wait("a", made["opc"], i_w1, i_w2)
        rp = did(g.scalar.activation(T.RP[:, :], T.IW[:, :].indirect(T.OPC[:, :]), Copy))
        wait("a", rp, made["osc"])
        did(g.scalar.activation(T.CM[:, :], T.RP[:, :].indirect(T.OS[:, 16:32]), Copy), 1, cm)

    k0 = fresh()
    wait("v", xa)
    did(g.vector.quantize_mx(T.KA[:, 0:128], T.PA[:, 0:128], T.XB[:, 0:512]), 1, k0)
    wait("v", "lx0")
    did(g.vector.quantize_mx(T.KA[:, 128:256], T.PA[:, 128:256], T.XB[:, 512:1024]), 1, k0)
    wait("v", "lsl")
    os_ = did(g.vector.tensor_copy(T.OS[:, 0:16], T.SLI[:, 0:16]))
    exchange(1, (T.KA[:, :], T.PA[:, :]), T.OS, 0, ([os_, k0], [os_, k0]),
             {(CODES, 1): parents, (CODES, 3): later_slots, (SCALES, 1): compose})

    q0 = did(g.vector.quantize_mx(T.W1[:, 0:256], T.P1[:, 0:256], piece(0)))
    wait("v", "lx1")
    x1 = did(g.vector.quantize_mx(T.W1[:, 512:768], T.P1[:, 512:768], piece(1)))
    wait("v", cm, a_step)
    sc = did(g.vector.tensor_tensor_scan(T.SC[:, :], T.step[:, :], T.CM[:, :], 0.0, AluOpType.add, AluOpType.max))

    def offsets(i, half):
        name = fresh()
        wait("v", sc, v_lf)
        for to in (LO, HI):
            did(g.vector.tensor_scalar(T.CO[to, NO * i:NO * i + NO], T.SC[half, 15:CW:16], T.lf[half, 0:1], None, AluOpType.subtract), 1, name)
        return name

    co2 = offsets(0, LO)
    dma("s", T.WB[:, 1536:2048], T.w[:, 1536:2048], "lwb", ["le1"])

    d = [q0, x1, co2]

    def later_lists():
        made["pa"] = halves(T.OP, T.par[LO, :], T.par[LO, :], [n2])
        made["co3"] = offsets(1, HI)

    exchange(2, (T.W1[:, :], T.P1[:, :]), T.CO, 0, (d + ["ac1"], d + ["as1"]), {(CODES, 3): later_lists})

    lwc = dma("s", T.WB[:, 1024:1536], T.w[:, 1024:1536], None, ["le2"])
    pa, co3 = made["pa"], made["co3"]
    k1c = pick("v", CODES, T.W1[:, :], T.OP[:, 0:16], T.W2[:, 0:CW], [pa])
    wait("v", "lwa")
    wqa = did(g.vector.quantize_mx(T.WQ[:, 0:256], T.WP[:, 0:256], T.WB[:, 0:1024]))
    wait("v", "lx2")
    x2 = did(g.vector.quantize_mx(T.W2[:, 512:768], T.P2[:, 512:768], piece(2)))
    k1s = pick("a", SCALES, T.P1[:, :], T.OP[:, 0:16], T.P2[:, 0:CW], [pa])
    own = T.OS[:, 2 * r:2 * r + 2]
    fs = pick("a", SCALES, T.PA[:, :], own, T.P3[:, at:at + SLOT], [])
    m0 = product(T.ps0[:, 0:CW], 0, T.W1[:, 0:CW], T.P1[:, 0:CW], [wqa, q0])
    m1 = product(T.ps1[:, 0:CW], 1, T.W2[:, 0:CW], T.P2[:, 0:CW], [k1c, k1s])
    wait("a", m0)
    y0 = did(g.scalar.activation(T.Y[:, 0:256], T.ps0[:, 0:256], Copy))
    wait("a", m1)
    y1 = did(g.scalar.activation(T.Y[:, 256:512], T.ps1[:, 0:256], Copy))

    exchange(3, (T.W2[:, :], T.P2[:, :]), T.CO, NO, ([k1c, x2, co3, "ac2"], [k1s, x2, co3, "as2"]))

    k2c = pick("v", CODES, T.W2[:, :], T.OP[:, 16:32], T.W3[:, 0:CW], [])
    k2s = pick("a", SCALES, T.P2[:, :], T.OP[:, 16:32], T.P3[:, 0:CW], [])
    x3 = did(g.vector.quantize_mx(T.W3[:, 512:768], T.P3[:, 512:768], piece(3)))
    wait("v", "lwb")
    wait("v", lwc)
    wqb = did(g.vector.quantize_mx(T.WQ[:, 256:512], T.WP[:, 256:512], T.WB[:, 1024:2048]))
    mn = product(T.ps5[:, 0:CW], 3, T.W3[:, 512:768], T.P3[:, 512:768], [wqb, x3])
    mo = product(T.ps6[:, 0:CW], 3, T.W3[:, 0:CW], T.P3[:, 0:CW], [k2c, k2s])
    m2 = product(T.ps2[:, 0:CW], 2, T.W3[:, 0:CW], T.P3[:, 0:CW], [])
    fc = pick("v", CODES, T.KA[:, :], own, T.W3[:, at:at + SLOT], [])
    wait("v", mn)
    zn = did(g.vector.tensor_copy(T.Z[:, 512:768], T.ps5[:, 0:256]))
    wait("a", mo)
    zo = did(g.scalar.activation(T.Z[:, 0:256], T.ps6[:, 0:256], Copy))
    wait("v", m2)
    y2 = did(g.vector.tensor_copy(T.Y[:, 512:768], T.ps2[:, 0:256]))
    st = [dma("s", T.y[:, 0:768], T.Y[:, 0:768], None, [y0, y1, y2, "le3"])]

    def slots(q, ps, a, b, n, deps):
        m = product(ps[:, 0:128], 3, T.W3[:, a:a + 128], T.P3[:, a:a + 128], deps)
        wait(q, m)
        if q == "v":
            return did(g.vector.tensor_copy(T.Z[:, b:b + n], ps[:, b - a:b - a + n]))
        return did(g.scalar.activation(T.Z[:, b:b + n], ps[:, b - a:b - a + n], Copy))

    home, other = CW + 64 * (r // 2), CW + 128 * (1 - r // 4)
    late = CW + 64 * ((r // 2) ^ 1)
    zh = slots("v", T.ps7, home - 64 if late > home else home, home, 64, [fc, fs, "ac3", "af3", "ap3"])
    za = slots("a", T.ps3, other, other, 128, ["ae3"])
    zb = slots("v", T.ps4, min(home, late), late, 64, ["as3"])
    wait("v", zo, zn, za, zh, zb)
    wait("a", zo, zn, za, zh, zb)
    for a in (768, 896):
        o = 32 + (a - 768) // 16
        ya = did(g.vector.tensor_copy(T.Y[:, a:a + 64], T.Z[:, :].indirect(T.OP[:, o:o + 4])))
        yb = did(g.scalar.activation(T.Y[:, a + 64:a + 128], T.Z[:, :].indirect(T.OP[:, o + 4:o + 8]), Copy))
        st.append(dma("s", T.y[:, a:a + 128], T.Y[:, a:a + 128], None, [ya, yb]))

    have = {n for (_, n) in waited}
    wait("g", *[n for n in total if n not in have and n not in st])
    wait("s", *st)
